import numpy as np
import ml_dtypes


def mxq(x, axis, fmt="e4m3"):
    dtype, down = {"e4m3": (ml_dtypes.float8_e4m3fn, 7), "e5m2": (ml_dtypes.float8_e5m2, 14)}[fmt]
    v = np.moveaxis(np.asarray(x, np.float32).astype(ml_dtypes.bfloat16).astype(np.float64), axis, -1)
    blocks = v.reshape(v.shape[:-1] + (-1, 32))
    amax = np.abs(blocks).max(-1, keepdims=True)
    byte = np.maximum(np.where(amax > 0, np.frexp(amax)[1] - 1 + 127, 0) - down, 1)
    scale = np.exp2(byte - 127.0)
    codes = (blocks / scale).astype(np.float32).astype(dtype).astype(np.float64)
    return np.moveaxis((codes * scale).reshape(v.shape), -1, axis)


WIDE = False


def mx_kscale(k):
    if not WIDE:
        return np.ones(k)
    levels = np.array([10, -10, 5, -5, 0])
    if k % 512:
        return np.exp2(np.random.permutation(np.resize(levels, k // 32))).repeat(32)
    a = np.empty((k // 512, 16))
    for p in range(k // 512):
        a[p, :8] = np.random.permutation(np.resize(levels, 8))
        for g in range(8):
            far = levels[np.abs(levels - a[p, g]) >= 10]
            a[p, g + 8] = far[np.random.randint(len(far))]
    return np.exp2(a.ravel()).repeat(32)


BF16 = ml_dtypes.bfloat16


def bf(x):
    return np.asarray(x, np.float32).astype(BF16)


def f64(x):
    return np.asarray(x).astype(np.float64)


E2M1 = np.array([0.0, 0.5, 1.0, 1.5, 2.0, 3.0, 4.0, 6.0, -0.0, -0.5, -1.0, -1.5, -2.0, -3.0, -4.0, -6.0])


def pack_weight(w, fmt):
    k, n = w.shape
    w = f64(bf(w)).reshape(k // 32, 32, n)
    amax = np.abs(w).max(1)
    if fmt == "e4m3":
        byte = np.frexp(amax)[1] - 1 + 127 - 7
    else:
        mant, ex = np.frexp(amax / 6.0)
        byte = np.where(mant > 0.5, ex, ex - 1) + 127
    byte = np.clip(np.where(amax > 0, byte, 1), 1, 254)
    scaled = (w * np.exp2(127.0 - byte)[:, None, :]).reshape(k, n).astype(np.float32)
    by_word = np.ascontiguousarray(scaled.reshape(k // 512, 128, 4, n).transpose(0, 1, 3, 2))
    if fmt == "e4m3":
        words = by_word.astype(ml_dtypes.float8_e4m3fn).view(np.uint8)
    else:
        c = by_word.astype(ml_dtypes.float4_e2m1fn).view(np.uint8) & 0xF
        words = c[..., 0::2] | (c[..., 1::2] << 4)
    return np.ascontiguousarray(words), np.ascontiguousarray(byte.astype(np.uint8).reshape(k // 512, 16, n))


def unpack_weight(words, scales, fmt):
    g, p, n, _ = words.shape
    if fmt == "e4m3":
        vals = np.ascontiguousarray(words).view(ml_dtypes.float8_e4m3fn).astype(np.float64)
    else:
        nib = np.empty((g, p, n, 4), np.uint8)
        nib[..., 0::2] = words & 0xF
        nib[..., 1::2] = words >> 4
        vals = E2M1[nib]
    vals = vals * np.repeat(np.exp2(scales.astype(np.float64) - 127.0), 8, axis=1)[..., None]
    return vals.transpose(0, 1, 3, 2).reshape(g * 512, n)
def pack4(w):
    words, scales = pack_weight(w, "e2m1")
    return words.reshape(words.shape[0], 128, -1), scales


def unpack4(words, scales):
    return unpack_weight(words.reshape(words.shape[0], 128, -1, 2), scales, "e2m1")


def planes(Y):
    n, m = Y.shape
    b = f64(bf(Y)).reshape(n // 32, 32, m)
    amax = np.abs(b).max(1)
    byte = np.clip(np.where(amax > 0, np.frexp(amax)[1] - 1 + 127 - 7, 1), 1, 254)
    codes = (b * np.exp2(127.0 - byte)[:, None, :]).reshape(n, m).astype(np.float32).astype(ml_dtypes.float8_e4m3fn).view(np.uint8)
    words = codes.reshape(n // 512, 128, 4, m).transpose(0, 1, 3, 2)
    return np.ascontiguousarray(words), np.ascontiguousarray(byte.astype(np.uint8).reshape(n // 512, 16, m))


D, MU, MV = 1536, 1024, 512

CORR = 0.33


def setup_inputs():
    s = mx_kscale(D)
    t = mx_kscale(D)
    X = np.random.randn(D, MV) * s[:, None]
    F = CORR * np.random.randn(D, D) / np.sqrt(D) / s[:, None] * s[None, :]
    E = CORR * np.random.randn(D, D) / np.sqrt(D) / s[:, None] * s[None, :]
    w = np.exp(0.4 * np.random.randn(D)) * t / s
    U = np.random.randn(D, MU) / np.sqrt(D) / t[:, None]
    gain = np.exp(0.8 * np.random.randn(MU))
    x_words, x_scales = pack_weight(X, "e4m3")
    f_words, f_scales = pack4(F)
    return {"x_words": x_words, "x_scales": x_scales, "f_words": f_words, "f_scales": f_scales,
            "E": bf(E), "w": bf(w), "U": bf(U), "gain": bf(gain)}


def reference(x_words, x_scales, f_words, f_scales, E, w, U, gain):
    x = unpack_weight(x_words, x_scales, "e4m3")
    f = unpack4(f_words, f_scales)
    z1 = x + (f.T @ x)
    z2 = z1 + (mxq(f64(E), 0, "e4m3").T @ mxq(z1, 0, "e4m3"))
    z = f64(w)[:, None] * z2
    c = mxq(f64(U), 0, "e4m3").T @ mxq(z, 0, "e4m3")
    y = c * f64(gain)[:, None]
    Y = y
    words, scales = planes(Y)
    return y, words, scales

@@ -1,0 +1,417 @@
+from contextlib import ExitStack
+
+import concourse.mybir as mybir
+from concourse.masks import make_identity
+
+D, MU, MV = 1536, 1024, 512
+FLOPS = 2 * D * MV * (D + D + MU)
+
+F32 = mybir.dt.float32
+BF16 = mybir.dt.bfloat16
+I32 = mybir.dt.int32
+U32 = mybir.dt.uint32
+U8 = mybir.dt.uint8
+FP8X4 = mybir.dt.float8_e4m3fn_x4
+FP4X4 = mybir.dt.float4_e2m1fn_x4
+ALU = mybir.AluOpType
+ACT = mybir.ActivationFunctionType
+
+P = 128
+G = 512
+NG = D // G
+NI = MU // G
+HALF = MV // 2
+QUARTER = MV // 4
+
+
+def tile_cross_block_rayleigh_coefficients_k1_kernel(
+    tc, x_words, x_scales, f_words, f_scales, E, w, U, gain, out_0, out_1, out_2
+):
+    nc = tc.nc
+    with ExitStack() as ctx:
+        keep = ctx.enter_context(tc.tile_pool(name="keep", bufs=1))
+        stage = ctx.enter_context(tc.tile_pool(name="stage", bufs=5))
+        psum = ctx.enter_context(tc.psum_pool(name="psum", bufs=8))
+        ctx.enter_context(tc.manual_schedule())
+
+        def kept(shape, dtype, name):
+            return keep.tile(shape, dtype, name=name, align_bytes=64)
+
+        def operand(width, name):
+            return kept([P, width], U32, name + "_codes"), kept([P, width], U8, name + "_scales")
+
+        w_rows = kept([P, NG * P], BF16, "w_rows")
+        w_col = kept([P, NG, 4], F32, "w_col")
+        gain_raw = kept([P, NI, 4], BF16, "gain_raw")
+        gain_col = kept([P, NI, 4], F32, "gain_col")
+        ident = kept([P, P], BF16, "ident")
+        f_raw = [kept([P, NG, 256], I32, "f_raw%d" % b) for b in range(NG)]
+        f_codes = [kept([P, NG, 1024], U8, "f_codes%d" % b) for b in range(NG)]
+        fs_first = kept([P, NG, G // 4], I32, "fs_first")
+        fs_rest = kept([P, NG, (D - G) // 4], I32, "fs_rest")
+        f_sc = [kept([P, NG, G], U8, "f_sc%d" % b) for b in range(NG)]
+        x_codes = [kept([P, NG, HALF], U32, "x_codes%d" % h) for h in range(2)]
+        x_sc = kept([P, NG, MV], U8, "x_sc")
+        e_cuts = [(0, 0, 2), (0, 2, 3), (1, 0, 1), (1, 1, 3), (2, 0, 3)]
+        e_rows = {cut: kept([P, 4, G * (cut[2] - cut[1])], BF16, "e_rows%d%d%d" % cut) for cut in e_cuts}
+        u_rows = [kept([P, 4, MU], BF16, "u_rows%d" % g) for g in range(NG)]
+        pick_q = operand(G, "pick")
+        e_q = {(g, b): operand(G, "e%d%d" % (g, b)) for g in range(NG) for b in range(NG)}
+        u_q = {(g, i): operand(G, "u%d%d" % (g, i)) for g in range(NG) for i in range(NI)}
+        z1_q = {(b, h): operand(HALF, "z1%d%d" % (b, h)) for b in range(NG) for h in range(2)}
+        z_q = [operand(MV, "z%d" % b) for b in range(NG)]
+        wz1 = {(b, h): kept([P, 4, HALF], F32, "wz1%d%d" % (b, h)) for b in range(NG) for h in range(2)}
+        y = [kept([P, 4, MV], F32, "y%d" % i) for i in range(NI)]
+        y_codes = {(i, h): kept([P, HALF], U32, "y_codes%d%d" % (i, h)) for i in range(NI) for h in range(2)}
+        y_sc = kept([P, MV], U8, "y_sc")
+        staged = {}
+
+        make_identity(nc, ident[:])
+        pick = stage.tile([P, 4 * G], BF16, name="pick", tag="wide", align_bytes=64)
+        nc.vector.memset(x_sc[:].bitcast(I32), 0)
+        nc.vector.memset(fs_first[:], 0)
+        nc.vector.memset(w_rows[:], 0.0)
+        nc.vector.memset(pick[:], 0.0)
+        nc.vector.memset(fs_rest[:], 0)
+
+        f32w = f_words.bitcast(I32).rearrange("g p n -> p g n")
+        x32w = x_words.rearrange("g p n t -> g p (n t)").bitcast(I32).rearrange("g p n -> p g n")
+        fs32 = f_scales.bitcast(I32).rearrange("g (q r) n -> r q g n", r=4)
+        xs32 = x_scales.bitcast(I32).rearrange("g (q r) n -> r q g n", r=4)
+
+        def load_f(b):
+            nc.sync.dma_start(out=f_raw[b][:], in_=f32w[:, :, 256 * b : 256 * (b + 1)])
+
+        def load_x(h):
+            nc.sync.dma_start(out=x_codes[h][:].bitcast(I32), in_=x32w[:, :, HALF * h : HALF * (h + 1)])
+
+        def load_rows(dst, src, g, c0, c1):
+            rows = src[G * g : G * (g + 1), c0:c1].rearrange("(a t b) c -> t a b c", t=4, b=4)
+            for t in range(4):
+                nc.sync.dma_start(out=dst[:, t, :], in_=rows[t])
+
+        def load_e(n):
+            g, b0, b1 = e_cuts[n]
+            load_rows(e_rows[e_cuts[n]], E, g, G * b0, G * b1)
+
+        def load_fs(dst, c0, c1):
+            for r in range(4):
+                nc.sync.dma_start(out=dst[r:P:32, :, :], in_=fs32[r][:, :, c0:c1])
+
+        def load_xs(r):
+            nc.sync.dma_start(out=x_sc[:].bitcast(I32)[r:P:32, :, :], in_=xs32[r])
+
+        for r in range(4):
+            load_xs(r)
+        load_f(0)
+        load_x(0)
+        load_fs(fs_first, 0, P)
+        load_e(0)
+        nc.sync.dma_start(
+            out=w_rows[0:4, :].rearrange("p (x b) -> p x b", b=4),
+            in_=w.rearrange("(x t b) -> t x b", t=4, b=4),
+        )
+        load_x(1)
+        load_e(1)
+        load_f(1)
+        load_fs(fs_rest, P, NG * P)
+        load_e(2)
+        load_e(3)
+        load_f(2)
+        load_e(4)
+        for g in range(NG):
+            load_rows(u_rows[g], U, g, 0, MU)
+        nc.sync.dma_start(out=gain_raw[:], in_=gain.rearrange("(i p t) -> p i t", p=P, t=4))
+
+        nc.vector.tensor_copy(
+            out=pick[:].rearrange("p (t a e) -> p t a e", t=4, e=16)[:, :, :, 0:16:5],
+            in_=ident[:].rearrange("p (a t) -> p t a", t=4).unsqueeze(3).to_broadcast([P, 4, 32, 4]),
+        )
+        nc.vector.quantize_mx(out=pick_q[0][:].bitcast(FP8X4), scales=pick_q[1][:], in_=pick[:])
+
+        def turn_w():
+            w_turned = psum.tile([P, NG, P], BF16, name="w_turned", tag="bank")
+            for g in range(NG):
+                nc.tensor.transpose(w_turned[:, g, :], w_rows[:, P * g : P * (g + 1)], ident[:])
+            nc.scalar.copy(out=w_col[:], in_=w_turned[:, :, 0:4])
+
+        def quantize(dst, src):
+            nc.vector.quantize_mx(out=dst[0][:].bitcast(FP8X4), scales=dst[1][:], in_=src)
+
+        def copy_on(engine, out, in_):
+            if engine == "vector":
+                nc.vector.tensor_copy(out=out, in_=in_)
+            else:
+                nc.scalar.copy(out=out, in_=in_)
+
+        def sort_f(b):
+            sort_f_codes(b)
+            sort_f_scales(b)
+
+        def sort_f_codes(b):
+            nc.vector.tensor_copy(
+                out=f_codes[b][:].bitcast(I32).rearrange("p g (t a v) -> p g t a v", t=4, v=2),
+                in_=f_raw[b][:].rearrange("p g (a t v) -> p g t a v", t=4, v=2),
+            )
+
+        def sort_f_scales(b):
+            nc.vector.tensor_copy(
+                out=f_sc[b][:].bitcast(I32).rearrange("p g (t c a) -> p g c t a", t=4, a=4),
+                in_=(fs_first[:] if b == 0 else fs_rest[:, :, P * (b - 1) : P * b]).rearrange("p g (c a t) -> p g c t a", t=4, a=4),
+            )
+
+        def e_source(g, b):
+            cut = [c for c in e_cuts if c[0] == g and c[1] <= b < c[2]][0]
+            return e_rows[cut][:, :, G * (b - cut[1]) : G * (b - cut[1] + 1)]
+
+        def lay_e(engine, g, b, t0=0, t1=4):
+            if t0 == 0:
+                staged["e", g, b] = stage.tile([P, 4 * G], BF16, name="wide", tag="wide", align_bytes=64)
+            dst = staged["e", g, b][:].rearrange("p (t a b j) -> p t a j b", t=4, b=4, j=4)
+            src = e_source(g, b).rearrange("p j (a t b) -> p t a j b", t=4, b=4)
+            copy_on(engine, dst[:, t0:t1], src[:, t0:t1])
+
+        def quant_e(g, b):
+            quantize(e_q[g, b], staged["e", g, b][:])
+
+        def lay_u(engine, g, i, t0=0, t1=4):
+            if t0 == 0:
+                staged["u", g, i] = stage.tile([P, 4 * G], BF16, name="wide", tag="wide", align_bytes=64)
+            dst = staged["u", g, i][:].rearrange("p (t c m j) -> p c t m j", t=4, m=2, j=4)
+            src = u_rows[g][:, :, G * i : G * (i + 1)].rearrange("p j (c m t) -> p c t m j", t=4, m=2)
+            copy_on(engine, dst[:, :, t0:t1], src[:, :, t0:t1])
+
+        def quant_u(g, i):
+            quantize(u_q[g, i], staged["u", g, i][:])
+
+        def first_product(b, h):
+            z1_words = stage.tile([P, HALF, 4], BF16, name="narrow", tag="narrow", align_bytes=64)
+            staged["z1", b, h] = z1_words
+            for q in range(2):
+                cols = slice(QUARTER * q, QUARTER * (q + 1))
+                xcols = slice(HALF * h + QUARTER * q, HALF * h + QUARTER * (q + 1))
+                bank = psum.tile([P, 4, QUARTER], F32, name="bank", tag="bank")
+                for t in range(4):
+                    for g in range(NG):
+                        nc.tensor.matmul_mx(
+                            out=bank[:, t, :],
+                            lhsT=f_codes[b][:, g, 256 * t : 256 * (t + 1)].bitcast(FP4X4),
+                            lhsT_scale=f_sc[b][:, g, P * t : P * (t + 1)],
+                            rhs=x_codes[h][:, g, cols].bitcast(FP8X4),
+                            rhs_scale=x_sc[:, g, xcols],
+                            start=(g == 0),
+                            stop=False,
+                        )
+                    nc.tensor.matmul_mx(
+                        out=bank[:, t, :],
+                        lhsT=pick_q[0][:, P * t : P * (t + 1)].bitcast(FP8X4),
+                        lhsT_scale=pick_q[1][:, P * t : P * (t + 1)],
+                        rhs=x_codes[h][:, b, cols].bitcast(FP8X4),
+                        rhs_scale=x_sc[:, b, xcols],
+                        start=False,
+                        stop=True,
+                    )
+                nc.scalar.copy(out=z1_words[:, cols, :], in_=bank[:].rearrange("p t n -> p n t"))
+                if (b, h, q) == (0, 0, 0):
+                    turn_w()
+                for t in range(4):
+                    nc.scalar.activation(
+                        out=wz1[b, h][:, t, cols], in_=bank[:, t, :], func=ACT.Copy, scale=w_col[:, b, t : t + 1]
+                    )
+
+        def quant_z1(b, h):
+            quantize(z1_q[b, h], staged["z1", b, h][:].rearrange("p n t -> p (n t)"))
+
+        def second_product(b, h):
+            for pair in range(2):
+                bank = psum.tile([P, 2, HALF], F32, name="bank", tag="bank")
+                staged["p2", b, h, pair] = bank
+                for s in range(2):
+                    t = 2 * pair + s
+                    for g in range(NG):
+                        nc.tensor.matmul_mx(
+                            out=bank[:, s, :],
+                            lhsT=e_q[g, b][0][:, P * t : P * (t + 1)].bitcast(FP8X4),
+                            lhsT_scale=e_q[g, b][1][:, P * t : P * (t + 1)],
+                            rhs=z1_q[g, h][0][:].bitcast(FP8X4),
+                            rhs_scale=z1_q[g, h][1][:],
+                            start=(g == 0),
+                            stop=(g == NG - 1),
+                        )
+
+        def third_passes(i, c0, c1, g0, g1):
+            for t in range(4):
+                if g1 - g0 == NG:
+                    if t % 2 == 0:
+                        bank = psum.tile([P, 2, c1 - c0], F32, name="bank", tag="bank")
+                    staged["p3", i, c0, t] = bank[:, t % 2, :]
+                elif g0 == 0:
+                    bank = psum.tile([P, c1 - c0], F32, name="bank", tag="bank")
+                    staged["p3", i, c0, t] = bank[:]
+                for g in range(g0, g1):
+                    nc.tensor.matmul_mx(
+                        out=staged["p3", i, c0, t],
+                        lhsT=u_q[g, i][0][:, P * t : P * (t + 1)].bitcast(FP8X4),
+                        lhsT_scale=u_q[g, i][1][:, P * t : P * (t + 1)],
+                        rhs=z_q[g][0][:, c0:c1].bitcast(FP8X4),
+                        rhs_scale=z_q[g][1][:, c0:c1],
+                        start=(g == 0),
+                        stop=(g == NG - 1),
+                    )
+
+        def finish_z(b, h):
+            z_slots = stage.tile([P, 4, HALF], BF16, name="z_slots", tag="z_slots", bufs=2, align_bytes=64)
+            staged["zs", b, h] = z_slots
+            for t in range(4):
+                nc.vector.scalar_tensor_tensor(
+                    out=z_slots[:, t, :],
+                    in0=staged["p2", b, h, t // 2][:, t % 2, :],
+                    scalar=w_col[:, b, t : t + 1],
+                    in1=wz1[b, h][:, t, :],
+                    op0=ALU.mult,
+                    op1=ALU.add,
+                )
+
+        def lay_slots(engine, key, slots):
+            staged[key] = stage.tile([P, HALF, 4], BF16, name="narrow", tag="narrow", align_bytes=64)
+            copy_on(
+                engine,
+                staged[key][:].rearrange("p (c n) t -> p c t n", n=4),
+                slots.rearrange("p t (c n) -> p c t n", n=4),
+            )
+
+        def lay_z(engine, b, h):
+            lay_slots(engine, ("z", b, h), staged["zs", b, h][:])
+
+        def quant_z(b, h):
+            cols = slice(HALF * h, HALF * (h + 1))
+            nc.vector.quantize_mx(
+                out=z_q[b][0][:, cols].bitcast(FP8X4),
+                scales=z_q[b][1][:, cols],
+                in_=staged["z", b, h][:].rearrange("p n t -> p (n t)"),
+            )
+
+        def finish_y(engine, i, c0, c1, t0, t1):
+            for t in range(t0, t1):
+                sums = staged["p3", i, c0, t]
+                if engine == "vector":
+                    nc.vector.tensor_scalar(
+                        out=y[i][:, t, c0:c1], in0=sums, scalar1=gain_col[:, i, t : t + 1], scalar2=None, op0=ALU.mult
+                    )
+                else:
+                    nc.scalar.activation(out=y[i][:, t, c0:c1], in_=sums, func=ACT.Copy, scale=gain_col[:, i, t : t + 1])
+            nc.sync.dma_start(
+                out=out_0[G * i : G * (i + 1), c0:c1].rearrange("(p t) m -> p t m", t=4)[:, t0:t1, :],
+                in_=y[i][:, t0:t1, c0:c1],
+            )
+
+        def lay_y(engine, i, h):
+            lay_slots(engine, ("y", i, h), y[i][:, :, HALF * h : HALF * (h + 1)])
+
+        def quant_y(i, h):
+            nc.vector.quantize_mx(
+                out=y_codes[i, h][:].bitcast(FP8X4),
+                scales=y_sc[4 * i : P, HALF * h : HALF * (h + 1)],
+                in_=staged["y", i, h][:].rearrange("p n t -> p (n t)"),
+            )
+            nc.sync.dma_start(
+                out=out_1[i].rearrange("p n t -> p (n t)").bitcast(I32)[:, HALF * h : HALF * (h + 1)],
+                in_=y_codes[i, h][:].bitcast(I32),
+            )
+
+        sort_f(0)
+        lay_e("scalar", 0, 1)
+        first_product(0, 0)
+        lay_e("vector", 0, 0)
+        quant_e(0, 0)
+        first_product(0, 1)
+        lay_e("vector", 0, 2)
+        quant_e(0, 1)
+        sort_f(1)
+        quant_e(0, 2)
+        quant_z1(0, 0)
+        first_product(1, 0)
+        lay_e("vector", 1, 0)
+        quant_z1(0, 1)
+        quant_e(1, 0)
+        first_product(1, 1)
+        lay_e("vector", 1, 1)
+        sort_f(2)
+        quant_e(1, 1)
+        lay_e("vector", 1, 2)
+        quant_z1(1, 0)
+        quant_e(1, 2)
+        first_product(2, 0)
+        lay_e("vector", 2, 0)
+        quant_z1(1, 1)
+        quant_e(2, 0)
+        first_product(2, 1)
+        lay_e("scalar", 2, 2)
+        lay_e("vector", 2, 1)
+        quant_z1(2, 0)
+        quant_e(2, 1)
+
+        second_product(0, 0)
+        second_product(1, 0)
+        lay_u("scalar", 0, 0)
+        quant_z1(2, 1)
+        finish_z(0, 0)
+        second_product(0, 1)
+        lay_z("vector", 0, 0)
+        finish_z(1, 0)
+        quant_e(2, 2)
+        second_product(2, 0)
+        lay_u("scalar", 1, 0)
+        quant_z(0, 0)
+        lay_z("vector", 1, 0)
+        finish_z(0, 1)
+        second_product(1, 1)
+        quant_z(1, 0)
+        quant_u(0, 0)
+        lay_u("scalar", 2, 0)
+        lay_z("vector", 0, 1)
+        finish_z(2, 0)
+        second_product(2, 1)
+        quant_z(0, 1)
+        quant_u(1, 0)
+        lay_z("vector", 2, 0)
+        lay_u("scalar", 0, 1)
+        finish_z(1, 1)
+        quant_z(2, 0)
+        quant_u(2, 0)
+        third_passes(0, 0, HALF, 0, NG)
+        lay_u("scalar", 1, 1, 0, 2)
+        nc.scalar.copy(out=gain_col[:], in_=gain_raw[:])
+        finish_y("scalar", 0, 0, HALF, 0, 4)
+        lay_u("scalar", 1, 1, 2, 4)
+        lay_z("vector", 1, 1)
+        finish_z(2, 1)
+        quant_z(1, 1)
+        quant_u(0, 1)
+        third_passes(0, HALF, MV, 0, NG - 1)
+        third_passes(1, 0, MV, 0, 1)
+        lay_z("vector", 2, 1)
+        lay_y("vector", 0, 0)
+        quant_z(2, 1)
+        quant_u(1, 1)
+        third_passes(0, HALF, MV, NG - 1, NG)
+        third_passes(1, 0, MV, 1, 2)
+        lay_u("scalar", 2, 1, 0, 2)
+        lay_u("vector", 2, 1, 2, 4)
+        quant_y(0, 0)
+        quant_u(2, 1)
+        third_passes(1, 0, MV, NG - 1, NG)
+        finish_y("scalar", 0, HALF, MV, 0, 4)
+        lay_y("vector", 0, 1)
+        finish_y("scalar", 1, 0, MV, 0, 2)
+        finish_y("vector", 1, 0, MV, 2, 4)
+        quant_y(0, 1)
+        lay_y("scalar", 1, 1)
+        lay_y("vector", 1, 0)
+        quant_y(1, 0)
+        quant_y(1, 1)
+        for q in range(4):
+            nc.sync.dma_start(
+                out=out_2.bitcast(I32)[:, 4 * q : 4 * (q + 1), :],
+                in_=y_sc[32 * q : 32 * q + 4 * NI, :].bitcast(I32),
+            )

@@ -40,15 +40,15 @@ def tile_cross_block_rayleigh_coefficients_k1_kernel(
         def operand(width, name):
             return kept([P, width], U32, name + "_codes"), kept([P, width], U8, name + "_scales")
 
-        w_rows = kept([P, NG * P], BF16, "w_rows")
-        w_col = kept([P, NG, 4], F32, "w_col")
+        w_raw = kept([NG, G], BF16, "w_raw")
+        w_rows = kept([P, G], BF16, "w_rows")
+        w_col = kept([P, 4, NG], F32, "w_col")
         gain_raw = kept([P, NI, 4], BF16, "gain_raw")
         gain_col = kept([P, NI, 4], F32, "gain_col")
         ident = kept([P, P], BF16, "ident")
         f_raw = [kept([P, NG, 256], I32, "f_raw%d" % b) for b in range(NG)]
         f_codes = [kept([P, NG, 1024], U8, "f_codes%d" % b) for b in range(NG)]
-        fs_first = kept([P, NG, G // 4], I32, "fs_first")
-        fs_rest = kept([P, NG, (D - G) // 4], I32, "fs_rest")
+        fs_raw = kept([P, NG, D // 4], I32, "fs_raw")
         f_sc = [kept([P, NG, G], U8, "f_sc%d" % b) for b in range(NG)]
         x_codes = [kept([P, NG, HALF], U32, "x_codes%d" % h) for h in range(2)]
         x_sc = kept([P, NG, MV], U8, "x_sc")
@@ -67,12 +67,12 @@ def tile_cross_block_rayleigh_coefficients_k1_kernel(
         staged = {}
 
         make_identity(nc, ident[:])
+        nc.gpsimd.dma_start(out=w_raw[:], in_=w.rearrange("(g k) -> g k", g=NG))
         pick = stage.tile([P, 4 * G], BF16, name="pick", tag="wide", align_bytes=64)
         nc.vector.memset(x_sc[:].bitcast(I32), 0)
-        nc.vector.memset(fs_first[:], 0)
-        nc.vector.memset(w_rows[:], 0.0)
+        nc.vector.memset(fs_raw[:], 0)
         nc.vector.memset(pick[:], 0.0)
-        nc.vector.memset(fs_rest[:], 0)
+        nc.vector.memset(w_rows[:], 0.0)
 
         f32w = f_words.bitcast(I32).rearrange("g p n -> p g n")
         x32w = x_words.rearrange("g p n t -> g p (n t)").bitcast(I32).rearrange("g p n -> p g n")
@@ -101,20 +101,15 @@ def tile_cross_block_rayleigh_coefficients_k1_kernel(
         def load_xs(r):
             nc.sync.dma_start(out=x_sc[:].bitcast(I32)[r:P:32, :, :], in_=xs32[r])
 
-        for r in range(4):
-            load_xs(r)
         load_f(0)
         load_x(0)
-        load_fs(fs_first, 0, P)
+        for r in range(4):
+            load_xs(r)
+        load_fs(fs_raw, 0, NG * P)
         load_e(0)
-        nc.sync.dma_start(
-            out=w_rows[0:4, :].rearrange("p (x b) -> p x b", b=4),
-            in_=w.rearrange("(x t b) -> t x b", t=4, b=4),
-        )
         load_x(1)
         load_e(1)
         load_f(1)
-        load_fs(fs_rest, P, NG * P)
         load_e(2)
         load_e(3)
         load_f(2)
@@ -128,12 +123,17 @@ def tile_cross_block_rayleigh_coefficients_k1_kernel(
             in_=ident[:].rearrange("p (a t) -> p t a", t=4).unsqueeze(3).to_broadcast([P, 4, 32, 4]),
         )
         nc.vector.quantize_mx(out=pick_q[0][:].bitcast(FP8X4), scales=pick_q[1][:], in_=pick[:])
+        nc.scalar.activation(
+            out=w_rows[0:NG, :].rearrange("p (t a b) -> p t a b", t=4, b=4),
+            in_=w_raw[:].rearrange("p (a t b) -> p t a b", t=4, b=4),
+            func=ACT.Copy,
+        )
 
         def turn_w():
-            w_turned = psum.tile([P, NG, P], BF16, name="w_turned", tag="bank")
-            for g in range(NG):
-                nc.tensor.transpose(w_turned[:, g, :], w_rows[:, P * g : P * (g + 1)], ident[:])
-            nc.scalar.copy(out=w_col[:], in_=w_turned[:, :, 0:4])
+            w_turned = psum.tile([P, 4, P], BF16, name="w_turned", tag="bank")
+            for t in range(4):
+                nc.tensor.transpose(w_turned[:, t, :], w_rows[:, P * t : P * (t + 1)], ident[:])
+            nc.scalar.copy(out=w_col[:], in_=w_turned[:, :, 0:NG])
 
         def quantize(dst, src):
             nc.vector.quantize_mx(out=dst[0][:].bitcast(FP8X4), scales=dst[1][:], in_=src)
@@ -157,7 +157,7 @@ def tile_cross_block_rayleigh_coefficients_k1_kernel(
         def sort_f_scales(b):
             nc.vector.tensor_copy(
                 out=f_sc[b][:].bitcast(I32).rearrange("p g (t c a) -> p g c t a", t=4, a=4),
-                in_=(fs_first[:] if b == 0 else fs_rest[:, :, P * (b - 1) : P * b]).rearrange("p g (c a t) -> p g c t a", t=4, a=4),
+                in_=fs_raw[:, :, P * b : P * (b + 1)].rearrange("p g (c a t) -> p g c t a", t=4, a=4),
             )
 
         def e_source(g, b):
@@ -216,7 +216,7 @@ def tile_cross_block_rayleigh_coefficients_k1_kernel(
                     turn_w()
                 for t in range(4):
                     nc.scalar.activation(
-                        out=wz1[b, h][:, t, cols], in_=bank[:, t, :], func=ACT.Copy, scale=w_col[:, b, t : t + 1]
+                        out=wz1[b, h][:, t, cols], in_=bank[:, t, :], func=ACT.Copy, scale=w_col[:, t, b : b + 1]
                     )
 
         def quant_z1(b, h):
@@ -266,7 +266,7 @@ def tile_cross_block_rayleigh_coefficients_k1_kernel(
                 nc.vector.scalar_tensor_tensor(
                     out=z_slots[:, t, :],
                     in0=staged["p2", b, h, t // 2][:, t % 2, :],
-                    scalar=w_col[:, b, t : t + 1],
+                    scalar=w_col[:, t, b : b + 1],
                     in1=wz1[b, h][:, t, :],
                     op0=ALU.mult,
                     op1=ALU.add,
@@ -411,7 +411,7 @@ def tile_cross_block_rayleigh_coefficients_k1_kernel(
         quant_y(1, 0)
         quant_y(1, 1)
         for q in range(4):
-            nc.sync.dma_start(
+            nc.scalar.dma_start(
                 out=out_2.bitcast(I32)[:, 4 * q : 4 * (q + 1), :],
                 in_=y_sc[32 * q : 32 * q + 4 * NI, :].bitcast(I32),
             )

@@ -17,11 +17,19 @@ ALU = mybir.AluOpType
 ACT = mybir.ActivationFunctionType
 
 P = 128
-G = 512
-NG = D // G
-NI = MU // G
+SLOTS = 4
+GROUP = P * SLOTS
+D_GROUPS = D // GROUP
+Y_GROUPS = MU // GROUP
 HALF = MV // 2
 QUARTER = MV // 4
+F_WORDS = GROUP // 2
+F_SLOT_BYTES = 2 * P
+SCALE_WORDS = GROUP // 4
+QUADRANT = 32
+STAGE_BUFS = 5
+E_LOADS = ((0, 0, 1), (0, 1, 2), (0, 2, 3), (1, 0, 1), (1, 1, 3), (2, 0, 3))
+Y_PIECES = ((0, 0, HALF), (0, HALF, MV), (1, 0, MV))
 
 
 def tile_cross_block_rayleigh_coefficients_k1_kernel(
@@ -30,113 +38,102 @@ def tile_cross_block_rayleigh_coefficients_k1_kernel(
     nc = tc.nc
     with ExitStack() as ctx:
         keep = ctx.enter_context(tc.tile_pool(name="keep", bufs=1))
-        stage = ctx.enter_context(tc.tile_pool(name="stage", bufs=5))
+        stage = ctx.enter_context(tc.tile_pool(name="stage", bufs=STAGE_BUFS))
         psum = ctx.enter_context(tc.psum_pool(name="psum", bufs=8))
         ctx.enter_context(tc.manual_schedule())
 
         def kept(shape, dtype, name):
             return keep.tile(shape, dtype, name=name, align_bytes=64)
 
-        def operand(width, name):
+        def mx_operand(width, name):
             return kept([P, width], U32, name + "_codes"), kept([P, width], U8, name + "_scales")
 
-        w_raw = kept([NG, G], BF16, "w_raw")
-        w_rows = kept([P, G], BF16, "w_rows")
-        w_col = kept([P, 4, NG], F32, "w_col")
-        gain_raw = kept([P, NI, 4], BF16, "gain_raw")
-        gain_col = kept([P, NI, 4], F32, "gain_col")
+        def weight_words():
+            return stage.tile([P, GROUP * SLOTS], BF16, name="weight_words", align_bytes=64)
+
+        def half_words():
+            return stage.tile([P, HALF, SLOTS], BF16, name="half_words", align_bytes=64)
+
+        def new_bank(shape, dtype):
+            return psum.tile(shape, dtype, name="bank")
+
+        groups = range(D_GROUPS)
+        halves = range(2)
+        slots = range(SLOTS)
+
         ident = kept([P, P], BF16, "ident")
-        f_raw = [kept([P, NG, 256], I32, "f_raw%d" % b) for b in range(NG)]
-        f_codes = [kept([P, NG, 1024], U8, "f_codes%d" % b) for b in range(NG)]
-        fs_raw = kept([P, NG, D // 4], I32, "fs_raw")
-        f_sc = [kept([P, NG, G], U8, "f_sc%d" % b) for b in range(NG)]
-        x_codes = [kept([P, NG, HALF], U32, "x_codes%d" % h) for h in range(2)]
-        x_sc = kept([P, NG, MV], U8, "x_sc")
-        e_cuts = [(0, 0, 2), (0, 2, 3), (1, 0, 1), (1, 1, 3), (2, 0, 3)]
-        e_rows = {cut: kept([P, 4, G * (cut[2] - cut[1])], BF16, "e_rows%d%d%d" % cut) for cut in e_cuts}
-        u_rows = [kept([P, 4, MU], BF16, "u_rows%d" % g) for g in range(NG)]
-        pick_q = operand(G, "pick")
-        e_q = {(g, b): operand(G, "e%d%d" % (g, b)) for g in range(NG) for b in range(NG)}
-        u_q = {(g, i): operand(G, "u%d%d" % (g, i)) for g in range(NG) for i in range(NI)}
-        z1_q = {(b, h): operand(HALF, "z1%d%d" % (b, h)) for b in range(NG) for h in range(2)}
-        z_q = [operand(MV, "z%d" % b) for b in range(NG)]
-        wz1 = {(b, h): kept([P, 4, HALF], F32, "wz1%d%d" % (b, h)) for b in range(NG) for h in range(2)}
-        y = [kept([P, 4, MV], F32, "y%d" % i) for i in range(NI)]
-        y_codes = {(i, h): kept([P, HALF], U32, "y_codes%d%d" % (i, h)) for i in range(NI) for h in range(2)}
-        y_sc = kept([P, MV], U8, "y_sc")
+        w_raw = kept([D_GROUPS, GROUP], BF16, "w_raw")
+        w_rows = kept([P, GROUP], BF16, "w_rows")
+        w_col = kept([P, SLOTS, D_GROUPS], F32, "w_col")
+        gain_raw = kept([P, Y_GROUPS, SLOTS], BF16, "gain_raw")
+        gain_col = kept([P, Y_GROUPS, SLOTS], F32, "gain_col")
+        f_raw = [kept([P, D_GROUPS, F_WORDS], I32, "f_raw%d" % b) for b in groups]
+        f_codes = [kept([P, D_GROUPS, 4 * F_WORDS], U8, "f_codes%d" % b) for b in groups]
+        f_planes_raw = kept([P, D_GROUPS, D // 4], I32, "f_planes_raw")
+        f_planes = [kept([P, D_GROUPS, GROUP], U8, "f_planes%d" % b) for b in groups]
+        x_codes = [kept([P, D_GROUPS, HALF], U32, "x_codes%d" % h) for h in halves]
+        x_planes = kept([P, D_GROUPS, MV], U8, "x_planes")
+        e_rows = {ld: kept([P, SLOTS, GROUP * (ld[2] - ld[1])], BF16, "e_rows%d%d%d" % ld) for ld in E_LOADS}
+        u_rows = [kept([P, SLOTS, MU], BF16, "u_rows%d" % g) for g in groups]
+        pick_mx = mx_operand(GROUP, "pick")
+        e_mx = {(g, b): mx_operand(GROUP, "e%d%d" % (g, b)) for g in groups for b in groups}
+        u_mx = {(g, i): mx_operand(GROUP, "u%d%d" % (g, i)) for g in groups for i in range(Y_GROUPS)}
+        z1_mx = {(b, h): mx_operand(HALF, "z1%d%d" % (b, h)) for b in groups for h in halves}
+        z_mx = [mx_operand(MV, "z%d" % b) for b in groups]
+        w_z1 = {(b, h): kept([P, SLOTS, HALF], F32, "w_z1%d%d" % (b, h)) for b in groups for h in halves}
+        y = {pc[:2]: kept([P, SLOTS, pc[2] - pc[1]], F32, "y%d%d" % pc[:2]) for pc in Y_PIECES}
+        y_codes = {(i, h): kept([P, HALF], U32, "y_codes%d%d" % (i, h)) for i in range(Y_GROUPS) for h in halves}
+        y_planes = kept([P, MV], U8, "y_planes")
+        pick_words = weight_words()
         staged = {}
 
+        nc.gpsimd.dma_start(out=w_raw[:], in_=w.rearrange("(g k) -> g k", g=D_GROUPS))
         make_identity(nc, ident[:])
-        nc.gpsimd.dma_start(out=w_raw[:], in_=w.rearrange("(g k) -> g k", g=NG))
-        pick = stage.tile([P, 4 * G], BF16, name="pick", tag="wide", align_bytes=64)
-        nc.vector.memset(x_sc[:].bitcast(I32), 0)
-        nc.vector.memset(fs_raw[:], 0)
-        nc.vector.memset(pick[:], 0.0)
+        nc.vector.memset(x_planes[:].bitcast(I32), 0)
+        nc.vector.memset(f_planes_raw[:], 0)
+        nc.vector.memset(pick_words[:], 0.0)
         nc.vector.memset(w_rows[:], 0.0)
 
-        f32w = f_words.bitcast(I32).rearrange("g p n -> p g n")
-        x32w = x_words.rearrange("g p n t -> g p (n t)").bitcast(I32).rearrange("g p n -> p g n")
-        fs32 = f_scales.bitcast(I32).rearrange("g (q r) n -> r q g n", r=4)
-        xs32 = x_scales.bitcast(I32).rearrange("g (q r) n -> r q g n", r=4)
+        f_words32 = f_words.bitcast(I32).rearrange("g p n -> p g n")
+        x_words32 = x_words.rearrange("g p n t -> g p (n t)").bitcast(I32).rearrange("g p n -> p g n")
+        f_scales32 = f_scales.bitcast(I32).rearrange("g (q r) n -> r q g n", r=4)
+        x_scales32 = x_scales.bitcast(I32).rearrange("g (q r) n -> r q g n", r=4)
 
         def load_f(b):
-            nc.sync.dma_start(out=f_raw[b][:], in_=f32w[:, :, 256 * b : 256 * (b + 1)])
+            nc.sync.dma_start(out=f_raw[b][:], in_=f_words32[:, :, F_WORDS * b : F_WORDS * (b + 1)])
 
         def load_x(h):
-            nc.sync.dma_start(out=x_codes[h][:].bitcast(I32), in_=x32w[:, :, HALF * h : HALF * (h + 1)])
+            nc.sync.dma_start(out=x_codes[h][:].bitcast(I32), in_=x_words32[:, :, HALF * h : HALF * (h + 1)])
 
-        def load_rows(dst, src, g, c0, c1):
-            rows = src[G * g : G * (g + 1), c0:c1].rearrange("(a t b) c -> t a b c", t=4, b=4)
-            for t in range(4):
+        def load_rows(dst, src, g, col0, col1):
+            rows = src[GROUP * g : GROUP * (g + 1), col0:col1].rearrange("(a t b) c -> t a b c", t=SLOTS, b=4)
+            for t in slots:
                 nc.sync.dma_start(out=dst[:, t, :], in_=rows[t])
 
-        def load_e(n):
-            g, b0, b1 = e_cuts[n]
-            load_rows(e_rows[e_cuts[n]], E, g, G * b0, G * b1)
-
-        def load_fs(dst, c0, c1):
-            for r in range(4):
-                nc.sync.dma_start(out=dst[r:P:32, :, :], in_=fs32[r][:, :, c0:c1])
-
-        def load_xs(r):
-            nc.sync.dma_start(out=x_sc[:].bitcast(I32)[r:P:32, :, :], in_=xs32[r])
+        def load_e(ld):
+            load_rows(e_rows[ld], E, ld[0], GROUP * ld[1], GROUP * ld[2])
 
         load_f(0)
         load_x(0)
         for r in range(4):
-            load_xs(r)
-        load_fs(fs_raw, 0, NG * P)
-        load_e(0)
+            queue = nc.sync if r < 2 else nc.gpsimd
+            queue.dma_start(out=x_planes[:].bitcast(I32)[r:P:QUADRANT, :, :], in_=x_scales32[r])
+        for r in range(4):
+            nc.sync.dma_start(out=f_planes_raw[r:P:QUADRANT, :, :], in_=f_scales32[r])
+        for ld in E_LOADS[0:3]:
+            load_e(ld)
         load_x(1)
-        load_e(1)
         load_f(1)
-        load_e(2)
-        load_e(3)
+        for ld in E_LOADS[3:5]:
+            load_e(ld)
         load_f(2)
-        load_e(4)
-        for g in range(NG):
+        load_e(E_LOADS[5])
+        for g in groups:
             load_rows(u_rows[g], U, g, 0, MU)
-        nc.sync.dma_start(out=gain_raw[:], in_=gain.rearrange("(i p t) -> p i t", p=P, t=4))
+        nc.sync.dma_start(out=gain_raw[:], in_=gain.rearrange("(i p t) -> p i t", p=P, t=SLOTS))
 
-        nc.vector.tensor_copy(
-            out=pick[:].rearrange("p (t a e) -> p t a e", t=4, e=16)[:, :, :, 0:16:5],
-            in_=ident[:].rearrange("p (a t) -> p t a", t=4).unsqueeze(3).to_broadcast([P, 4, 32, 4]),
-        )
-        nc.vector.quantize_mx(out=pick_q[0][:].bitcast(FP8X4), scales=pick_q[1][:], in_=pick[:])
-        nc.scalar.activation(
-            out=w_rows[0:NG, :].rearrange("p (t a b) -> p t a b", t=4, b=4),
-            in_=w_raw[:].rearrange("p (a t b) -> p t a b", t=4, b=4),
-            func=ACT.Copy,
-        )
-
-        def turn_w():
-            w_turned = psum.tile([P, 4, P], BF16, name="w_turned", tag="bank")
-            for t in range(4):
-                nc.tensor.transpose(w_turned[:, t, :], w_rows[:, P * t : P * (t + 1)], ident[:])
-            nc.scalar.copy(out=w_col[:], in_=w_turned[:, :, 0:NG])
-
-        def quantize(dst, src):
-            nc.vector.quantize_mx(out=dst[0][:].bitcast(FP8X4), scales=dst[1][:], in_=src)
+        def quantize(codes, scales, words):
+            nc.vector.quantize_mx(out=codes.bitcast(FP8X4), scales=scales, in_=words)
 
         def copy_on(engine, out, in_):
             if engine == "vector":
@@ -144,196 +141,202 @@ def tile_cross_block_rayleigh_coefficients_k1_kernel(
             else:
                 nc.scalar.copy(out=out, in_=in_)
 
-        def sort_f(b):
-            sort_f_codes(b)
-            sort_f_scales(b)
+        def mx_pass(out, weights, t, codes, scales, start, stop):
+            nc.tensor.matmul_mx(
+                out=out,
+                lhsT=weights[0][:, P * t : P * (t + 1)].bitcast(FP8X4),
+                lhsT_scale=weights[1][:, P * t : P * (t + 1)],
+                rhs=codes.bitcast(FP8X4),
+                rhs_scale=scales,
+                start=start,
+                stop=stop,
+            )
+
+        def make_pick():
+            nc.vector.tensor_copy(
+                out=pick_words[:].rearrange("p (t a e) -> p t a e", t=SLOTS, e=16)[:, :, :, 0:16:5],
+                in_=ident[:].rearrange("p (a t) -> p t a", t=SLOTS).unsqueeze(3).to_broadcast([P, SLOTS, 32, 4]),
+            )
+            quantize(pick_mx[0][:], pick_mx[1][:], pick_words[:])
+
+        def sort_w():
+            nc.scalar.activation(
+                out=w_rows[0:D_GROUPS, :].rearrange("p (t a b) -> p t a b", t=SLOTS, b=4),
+                in_=w_raw[:].rearrange("p (a t b) -> p t a b", t=SLOTS, b=4),
+                func=ACT.Copy,
+            )
+
+        def turn_w():
+            turned = new_bank([P, SLOTS, P], BF16)
+            for t in slots:
+                nc.tensor.transpose(turned[:, t, :], w_rows[:, P * t : P * (t + 1)], ident[:])
+            nc.scalar.copy(out=w_col[:], in_=turned[:, :, 0:D_GROUPS])
 
         def sort_f_codes(b):
             nc.vector.tensor_copy(
-                out=f_codes[b][:].bitcast(I32).rearrange("p g (t a v) -> p g t a v", t=4, v=2),
-                in_=f_raw[b][:].rearrange("p g (a t v) -> p g t a v", t=4, v=2),
+                out=f_codes[b][:].bitcast(I32).rearrange("p g (t a v) -> p g t a v", t=SLOTS, v=2),
+                in_=f_raw[b][:].rearrange("p g (a t v) -> p g t a v", t=SLOTS, v=2),
             )
 
-        def sort_f_scales(b):
+        def sort_f_planes(b):
+            raw = f_planes_raw[:, :, SCALE_WORDS * b : SCALE_WORDS * (b + 1)]
             nc.vector.tensor_copy(
-                out=f_sc[b][:].bitcast(I32).rearrange("p g (t c a) -> p g c t a", t=4, a=4),
-                in_=fs_raw[:, :, P * b : P * (b + 1)].rearrange("p g (c a t) -> p g c t a", t=4, a=4),
+                out=f_planes[b][:].bitcast(I32).rearrange("p g (t c m) -> p g c t m", t=SLOTS, m=4),
+                in_=raw.rearrange("p g (c m t) -> p g c t m", t=SLOTS, m=4),
             )
 
-        def e_source(g, b):
-            cut = [c for c in e_cuts if c[0] == g and c[1] <= b < c[2]][0]
-            return e_rows[cut][:, :, G * (b - cut[1]) : G * (b - cut[1] + 1)]
+        def sort_f(b):
+            sort_f_codes(b)
+            sort_f_planes(b)
 
-        def lay_e(engine, g, b, t0=0, t1=4):
-            if t0 == 0:
-                staged["e", g, b] = stage.tile([P, 4 * G], BF16, name="wide", tag="wide", align_bytes=64)
-            dst = staged["e", g, b][:].rearrange("p (t a b j) -> p t a j b", t=4, b=4, j=4)
-            src = e_source(g, b).rearrange("p j (a t b) -> p t a j b", t=4, b=4)
-            copy_on(engine, dst[:, t0:t1], src[:, t0:t1])
+        def lay_e(engine, g, b):
+            ld = [x for x in E_LOADS if x[0] == g and x[1] <= b < x[2]][0]
+            rows = e_rows[ld][:, :, GROUP * (b - ld[1]) : GROUP * (b - ld[1] + 1)]
+            staged["e", g, b] = weight_words()
+            copy_on(
+                engine,
+                staged["e", g, b][:].rearrange("p (t a b j) -> p t a j b", t=SLOTS, b=4, j=SLOTS),
+                rows.rearrange("p j (a t b) -> p t a j b", t=SLOTS, b=4),
+            )
 
         def quant_e(g, b):
-            quantize(e_q[g, b], staged["e", g, b][:])
+            quantize(e_mx[g, b][0][:], e_mx[g, b][1][:], staged["e", g, b][:])
 
-        def lay_u(engine, g, i, t0=0, t1=4):
+        def lay_u(engine, g, i, t0=0, t1=SLOTS):
             if t0 == 0:
-                staged["u", g, i] = stage.tile([P, 4 * G], BF16, name="wide", tag="wide", align_bytes=64)
-            dst = staged["u", g, i][:].rearrange("p (t c m j) -> p c t m j", t=4, m=2, j=4)
-            src = u_rows[g][:, :, G * i : G * (i + 1)].rearrange("p j (c m t) -> p c t m j", t=4, m=2)
+                staged["u", g, i] = weight_words()
+            dst = staged["u", g, i][:].rearrange("p (t c m j) -> p c t m j", t=SLOTS, m=2, j=SLOTS)
+            src = u_rows[g][:, :, GROUP * i : GROUP * (i + 1)].rearrange("p j (c m t) -> p c t m j", t=SLOTS, m=2)
             copy_on(engine, dst[:, :, t0:t1], src[:, :, t0:t1])
 
         def quant_u(g, i):
-            quantize(u_q[g, i], staged["u", g, i][:])
+            quantize(u_mx[g, i][0][:], u_mx[g, i][1][:], staged["u", g, i][:])
 
         def first_product(b, h):
-            z1_words = stage.tile([P, HALF, 4], BF16, name="narrow", tag="narrow", align_bytes=64)
+            z1_words = half_words()
             staged["z1", b, h] = z1_words
             for q in range(2):
                 cols = slice(QUARTER * q, QUARTER * (q + 1))
-                xcols = slice(HALF * h + QUARTER * q, HALF * h + QUARTER * (q + 1))
-                bank = psum.tile([P, 4, QUARTER], F32, name="bank", tag="bank")
-                for t in range(4):
-                    for g in range(NG):
+                x_cols = slice(HALF * h + cols.start, HALF * h + cols.stop)
+                bank = new_bank([P, SLOTS, QUARTER], F32)
+                for t in slots:
+                    for g in groups:
                         nc.tensor.matmul_mx(
                             out=bank[:, t, :],
-                            lhsT=f_codes[b][:, g, 256 * t : 256 * (t + 1)].bitcast(FP4X4),
-                            lhsT_scale=f_sc[b][:, g, P * t : P * (t + 1)],
+                            lhsT=f_codes[b][:, g, F_SLOT_BYTES * t : F_SLOT_BYTES * (t + 1)].bitcast(FP4X4),
+                            lhsT_scale=f_planes[b][:, g, P * t : P * (t + 1)],
                             rhs=x_codes[h][:, g, cols].bitcast(FP8X4),
-                            rhs_scale=x_sc[:, g, xcols],
+                            rhs_scale=x_planes[:, g, x_cols],
                             start=(g == 0),
                             stop=False,
                         )
-                    nc.tensor.matmul_mx(
-                        out=bank[:, t, :],
-                        lhsT=pick_q[0][:, P * t : P * (t + 1)].bitcast(FP8X4),
-                        lhsT_scale=pick_q[1][:, P * t : P * (t + 1)],
-                        rhs=x_codes[h][:, b, cols].bitcast(FP8X4),
-                        rhs_scale=x_sc[:, b, xcols],
-                        start=False,
-                        stop=True,
-                    )
+                    mx_pass(bank[:, t, :], pick_mx, t, x_codes[h][:, b, cols], x_planes[:, b, x_cols], False, True)
                 nc.scalar.copy(out=z1_words[:, cols, :], in_=bank[:].rearrange("p t n -> p n t"))
                 if (b, h, q) == (0, 0, 0):
                     turn_w()
-                for t in range(4):
+                for t in slots:
                     nc.scalar.activation(
-                        out=wz1[b, h][:, t, cols], in_=bank[:, t, :], func=ACT.Copy, scale=w_col[:, t, b : b + 1]
+                        out=w_z1[b, h][:, t, cols], in_=bank[:, t, :], func=ACT.Copy, scale=w_col[:, t, b : b + 1]
                     )
 
         def quant_z1(b, h):
-            quantize(z1_q[b, h], staged["z1", b, h][:].rearrange("p n t -> p (n t)"))
+            quantize(z1_mx[b, h][0][:], z1_mx[b, h][1][:], staged["z1", b, h][:].rearrange("p n t -> p (n t)"))
 
         def second_product(b, h):
-            for pair in range(2):
-                bank = psum.tile([P, 2, HALF], F32, name="bank", tag="bank")
-                staged["p2", b, h, pair] = bank
-                for s in range(2):
-                    t = 2 * pair + s
-                    for g in range(NG):
-                        nc.tensor.matmul_mx(
-                            out=bank[:, s, :],
-                            lhsT=e_q[g, b][0][:, P * t : P * (t + 1)].bitcast(FP8X4),
-                            lhsT_scale=e_q[g, b][1][:, P * t : P * (t + 1)],
-                            rhs=z1_q[g, h][0][:].bitcast(FP8X4),
-                            rhs_scale=z1_q[g, h][1][:],
-                            start=(g == 0),
-                            stop=(g == NG - 1),
-                        )
-
-        def third_passes(i, c0, c1, g0, g1):
-            for t in range(4):
-                if g1 - g0 == NG:
-                    if t % 2 == 0:
-                        bank = psum.tile([P, 2, c1 - c0], F32, name="bank", tag="bank")
-                    staged["p3", i, c0, t] = bank[:, t % 2, :]
-                elif g0 == 0:
-                    bank = psum.tile([P, c1 - c0], F32, name="bank", tag="bank")
-                    staged["p3", i, c0, t] = bank[:]
-                for g in range(g0, g1):
-                    nc.tensor.matmul_mx(
-                        out=staged["p3", i, c0, t],
-                        lhsT=u_q[g, i][0][:, P * t : P * (t + 1)].bitcast(FP8X4),
-                        lhsT_scale=u_q[g, i][1][:, P * t : P * (t + 1)],
-                        rhs=z_q[g][0][:, c0:c1].bitcast(FP8X4),
-                        rhs_scale=z_q[g][1][:, c0:c1],
-                        start=(g == 0),
-                        stop=(g == NG - 1),
-                    )
+            for t in slots:
+                if t % 2 == 0:
+                    bank = new_bank([P, 2, HALF], F32)
+                staged["ez1", b, h, t] = bank[:, t % 2, :]
+                for g in groups:
+                    codes, scales = z1_mx[g, h]
+                    mx_pass(bank[:, t % 2, :], e_mx[g, b], t, codes[:], scales[:], g == 0, g == D_GROUPS - 1)
 
         def finish_z(b, h):
-            z_slots = stage.tile([P, 4, HALF], BF16, name="z_slots", tag="z_slots", bufs=2, align_bytes=64)
-            staged["zs", b, h] = z_slots
-            for t in range(4):
+            z_slots = stage.tile([P, SLOTS, HALF], BF16, name="z_slots", bufs=2, align_bytes=64)
+            staged["z_slots", b, h] = z_slots
+            for t in slots:
                 nc.vector.scalar_tensor_tensor(
                     out=z_slots[:, t, :],
-                    in0=staged["p2", b, h, t // 2][:, t % 2, :],
+                    in0=staged["ez1", b, h, t],
                     scalar=w_col[:, t, b : b + 1],
-                    in1=wz1[b, h][:, t, :],
+                    in1=w_z1[b, h][:, t, :],
                     op0=ALU.mult,
                     op1=ALU.add,
                 )
 
-        def lay_slots(engine, key, slots):
-            staged[key] = stage.tile([P, HALF, 4], BF16, name="narrow", tag="narrow", align_bytes=64)
+        def lay_slots(engine, key, by_slot):
+            staged[key] = half_words()
             copy_on(
                 engine,
                 staged[key][:].rearrange("p (c n) t -> p c t n", n=4),
-                slots.rearrange("p t (c n) -> p c t n", n=4),
+                by_slot.rearrange("p t (c n) -> p c t n", n=4),
             )
 
-        def lay_z(engine, b, h):
-            lay_slots(engine, ("z", b, h), staged["zs", b, h][:])
+        def lay_z(b, h):
+            lay_slots("vector", ("z", b, h), staged["z_slots", b, h][:])
 
         def quant_z(b, h):
             cols = slice(HALF * h, HALF * (h + 1))
-            nc.vector.quantize_mx(
-                out=z_q[b][0][:, cols].bitcast(FP8X4),
-                scales=z_q[b][1][:, cols],
-                in_=staged["z", b, h][:].rearrange("p n t -> p (n t)"),
-            )
+            quantize(z_mx[b][0][:, cols], z_mx[b][1][:, cols], staged["z", b, h][:].rearrange("p n t -> p (n t)"))
 
-        def finish_y(engine, i, c0, c1, t0, t1):
+        def third_product(piece, g0=0, g1=D_GROUPS):
+            i, col0, col1 = piece
+            for t in slots:
+                if g1 - g0 == D_GROUPS:
+                    if t % 2 == 0:
+                        bank = new_bank([P, 2, col1 - col0], F32)
+                    staged["uz", piece, t] = bank[:, t % 2, :]
+                elif g0 == 0:
+                    bank = new_bank([P, col1 - col0], F32)
+                    staged["uz", piece, t] = bank[:]
+                for g in range(g0, g1):
+                    codes, scales = z_mx[g][0][:, col0:col1], z_mx[g][1][:, col0:col1]
+                    mx_pass(staged["uz", piece, t], u_mx[g, i], t, codes, scales, g == 0, g == D_GROUPS - 1)
+
+        def finish_y(engine, piece, t0, t1):
+            i, col0, col1 = piece
             for t in range(t0, t1):
-                sums = staged["p3", i, c0, t]
+                out, sums, factor = y[i, col0][:, t, :], staged["uz", piece, t], gain_col[:, i, t : t + 1]
                 if engine == "vector":
-                    nc.vector.tensor_scalar(
-                        out=y[i][:, t, c0:c1], in0=sums, scalar1=gain_col[:, i, t : t + 1], scalar2=None, op0=ALU.mult
-                    )
+                    nc.vector.tensor_scalar(out=out, in0=sums, scalar1=factor, scalar2=None, op0=ALU.mult)
                 else:
-                    nc.scalar.activation(out=y[i][:, t, c0:c1], in_=sums, func=ACT.Copy, scale=gain_col[:, i, t : t + 1])
-            nc.sync.dma_start(
-                out=out_0[G * i : G * (i + 1), c0:c1].rearrange("(p t) m -> p t m", t=4)[:, t0:t1, :],
-                in_=y[i][:, t0:t1, c0:c1],
-            )
+                    nc.scalar.activation(out=out, in_=sums, func=ACT.Copy, scale=factor)
+            rows = out_0[GROUP * i : GROUP * (i + 1), col0:col1].rearrange("(p t) m -> p t m", t=SLOTS)
+            nc.sync.dma_start(out=rows[:, t0:t1, :], in_=y[i, col0][:, t0:t1, :])
 
         def lay_y(engine, i, h):
-            lay_slots(engine, ("y", i, h), y[i][:, :, HALF * h : HALF * (h + 1)])
+            col0 = [pc[1] for pc in Y_PIECES if pc[0] == i and pc[1] <= HALF * h < pc[2]][0]
+            lay_slots(engine, ("y", i, h), y[i, col0][:, :, HALF * h - col0 : HALF * (h + 1) - col0])
 
         def quant_y(i, h):
-            nc.vector.quantize_mx(
-                out=y_codes[i, h][:].bitcast(FP8X4),
-                scales=y_sc[4 * i : P, HALF * h : HALF * (h + 1)],
-                in_=staged["y", i, h][:].rearrange("p n t -> p (n t)"),
-            )
+            cols = slice(HALF * h, HALF * (h + 1))
+            quantize(y_codes[i, h][:], y_planes[4 * i : P, cols], staged["y", i, h][:].rearrange("p n t -> p (n t)"))
             nc.sync.dma_start(
-                out=out_1[i].rearrange("p n t -> p (n t)").bitcast(I32)[:, HALF * h : HALF * (h + 1)],
-                in_=y_codes[i, h][:].bitcast(I32),
+                out=out_1[i].rearrange("p n t -> p (n t)").bitcast(I32)[:, cols], in_=y_codes[i, h][:].bitcast(I32)
             )
 
-        sort_f(0)
+        sort_f_codes(0)
+        make_pick()
+        sort_f_planes(0)
+        sort_w()
         lay_e("scalar", 0, 1)
+
         first_product(0, 0)
         lay_e("vector", 0, 0)
         quant_e(0, 0)
+
         first_product(0, 1)
         lay_e("vector", 0, 2)
         quant_e(0, 1)
-        sort_f(1)
         quant_e(0, 2)
+        sort_f(1)
         quant_z1(0, 0)
+
         first_product(1, 0)
         lay_e("vector", 1, 0)
-        quant_z1(0, 1)
         quant_e(1, 0)
+        quant_z1(0, 1)
+
         first_product(1, 1)
         lay_e("vector", 1, 1)
         sort_f(2)
@@ -341,70 +344,60 @@ def tile_cross_block_rayleigh_coefficients_k1_kernel(
         lay_e("vector", 1, 2)
         quant_z1(1, 0)
         quant_e(1, 2)
+
         first_product(2, 0)
         lay_e("vector", 2, 0)
         quant_z1(1, 1)
         quant_e(2, 0)
+
         first_product(2, 1)
         lay_e("scalar", 2, 2)
         lay_e("vector", 2, 1)
         quant_z1(2, 0)
         quant_e(2, 1)
 
-        second_product(0, 0)
-        second_product(1, 0)
-        lay_u("scalar", 0, 0)
+        z_parts = [(0, 0), (1, 0), (0, 1), (1, 1), (2, 0), (2, 1)]
+        z_finish = [(0, 0), (1, 0), (0, 1), (2, 0), (1, 1), (2, 1)]
+        u_pieces = [(g, i) for i in range(Y_GROUPS) for g in groups]
+        y_left, y_right, y_last = Y_PIECES
+
+        second_product(*z_parts[0])
+        second_product(*z_parts[1])
         quant_z1(2, 1)
-        finish_z(0, 0)
-        second_product(0, 1)
-        lay_z("vector", 0, 0)
-        finish_z(1, 0)
-        quant_e(2, 2)
-        second_product(2, 0)
-        lay_u("scalar", 1, 0)
-        quant_z(0, 0)
-        lay_z("vector", 1, 0)
-        finish_z(0, 1)
-        second_product(1, 1)
-        quant_z(1, 0)
-        quant_u(0, 0)
-        lay_u("scalar", 2, 0)
-        lay_z("vector", 0, 1)
-        finish_z(2, 0)
-        second_product(2, 1)
-        quant_z(0, 1)
-        quant_u(1, 0)
-        lay_z("vector", 2, 0)
-        lay_u("scalar", 0, 1)
-        finish_z(1, 1)
-        quant_z(2, 0)
-        quant_u(2, 0)
-        third_passes(0, 0, HALF, 0, NG)
-        lay_u("scalar", 1, 1, 0, 2)
+        for n in range(len(z_finish)):
+            if n < len(u_pieces) - 1:
+                lay_u("scalar", *u_pieces[n])
+            finish_z(*z_finish[n])
+            if n > 0:
+                quant_z(*z_finish[n - 1])
+            if n == 1:
+                quant_e(2, 2)
+            if n > 1:
+                quant_u(*u_pieces[n - 2])
+            if n + 2 < len(z_parts):
+                second_product(*z_parts[n + 2])
+            if z_finish[n - 1] == (2, 0):
+                third_product(y_left)
+            lay_z(*z_finish[n])
+
+        third_product(y_last, 0, 1)
         nc.scalar.copy(out=gain_col[:], in_=gain_raw[:])
-        finish_y("scalar", 0, 0, HALF, 0, 4)
-        lay_u("scalar", 1, 1, 2, 4)
-        lay_z("vector", 1, 1)
-        finish_z(2, 1)
-        quant_z(1, 1)
-        quant_u(0, 1)
-        third_passes(0, HALF, MV, 0, NG - 1)
-        third_passes(1, 0, MV, 0, 1)
-        lay_z("vector", 2, 1)
-        lay_y("vector", 0, 0)
-        quant_z(2, 1)
+        finish_y("scalar", y_left, 0, SLOTS)
         quant_u(1, 1)
-        third_passes(0, HALF, MV, NG - 1, NG)
-        third_passes(1, 0, MV, 1, 2)
+        quant_z(2, 1)
+        third_product(y_right)
+        third_product(y_last, 1, 2)
         lay_u("scalar", 2, 1, 0, 2)
-        lay_u("vector", 2, 1, 2, 4)
-        quant_y(0, 0)
+        lay_u("vector", 2, 1, 2, SLOTS)
+        lay_y("vector", 0, 0)
         quant_u(2, 1)
-        third_passes(1, 0, MV, NG - 1, NG)
-        finish_y("scalar", 0, HALF, MV, 0, 4)
+        third_product(y_last, 2, D_GROUPS)
+        finish_y("scalar", y_right, 0, 2)
+        finish_y("scalar", y_right, 2, SLOTS)
+        quant_y(0, 0)
         lay_y("vector", 0, 1)
-        finish_y("scalar", 1, 0, MV, 0, 2)
-        finish_y("vector", 1, 0, MV, 2, 4)
+        finish_y("scalar", y_last, 0, 2)
+        finish_y("vector", y_last, 2, SLOTS)
         quant_y(0, 1)
         lay_y("scalar", 1, 1)
         lay_y("vector", 1, 0)
@@ -413,5 +406,5 @@ def tile_cross_block_rayleigh_coefficients_k1_kernel(
         for q in range(4):
             nc.scalar.dma_start(
                 out=out_2.bitcast(I32)[:, 4 * q : 4 * (q + 1), :],
-                in_=y_sc[32 * q : 32 * q + 4 * NI, :].bitcast(I32),
+                in_=y_planes[QUADRANT * q : QUADRANT * q + 4 * Y_GROUPS, :].bitcast(I32),
             )

@@ -28,7 +28,7 @@ F_SLOT_BYTES = 2 * P
 SCALE_WORDS = GROUP // 4
 QUADRANT = 32
 STAGE_BUFS = 5
-E_LOADS = ((0, 0, 1), (0, 1, 2), (0, 2, 3), (1, 0, 1), (1, 1, 3), (2, 0, 3))
+E_LOADS = ((0, 0, 1), (0, 1, 2), (0, 2, 3), (1, 0, 1), (1, 1, 2), (1, 2, 3), (2, 0, 1), (2, 1, 3))
 Y_PIECES = ((0, 0, HALF), (0, HALF, MV), (1, 0, MV))
 
 
@@ -127,7 +127,8 @@ def tile_cross_block_rayleigh_coefficients_k1_kernel(
         for ld in E_LOADS[3:5]:
             load_e(ld)
         load_f(2)
-        load_e(E_LOADS[5])
+        for ld in E_LOADS[5:]:
+            load_e(ld)
         for g in groups:
             load_rows(u_rows[g], U, g, 0, MU)
         nc.sync.dma_start(out=gain_raw[:], in_=gain.rearrange("(i p t) -> p i t", p=P, t=SLOTS))
@@ -205,9 +206,9 @@ def tile_cross_block_rayleigh_coefficients_k1_kernel(
         def lay_u(engine, g, i, t0=0, t1=SLOTS):
             if t0 == 0:
                 staged["u", g, i] = weight_words()
-            dst = staged["u", g, i][:].rearrange("p (t c m j) -> p c t m j", t=SLOTS, m=2, j=SLOTS)
-            src = u_rows[g][:, :, GROUP * i : GROUP * (i + 1)].rearrange("p j (c m t) -> p c t m j", t=SLOTS, m=2)
-            copy_on(engine, dst[:, :, t0:t1], src[:, :, t0:t1])
+            dst = staged["u", g, i][:].rearrange("p (t m j) -> p m j t", t=SLOTS, j=SLOTS)
+            src = u_rows[g][:, :, GROUP * i : GROUP * (i + 1)].rearrange("p j (m t) -> p m j t", t=SLOTS)
+            copy_on(engine, dst[:, :, :, t0:t1], src[:, :, :, t0:t1])
 
         def quant_u(g, i):
             quantize(u_mx[g, i][0][:], u_mx[g, i][1][:], staged["u", g, i][:])

from contextlib import ExitStack

import concourse.mybir as mybir
from concourse.masks import make_identity

D, MU, MV = 1536, 1024, 512
FLOPS = 2 * D * MV * (D + D + MU)

F32 = mybir.dt.float32
BF16 = mybir.dt.bfloat16
I32 = mybir.dt.int32
U32 = mybir.dt.uint32
U8 = mybir.dt.uint8
FP8X4 = mybir.dt.float8_e4m3fn_x4
FP4X4 = mybir.dt.float4_e2m1fn_x4
ALU = mybir.AluOpType
ACT = mybir.ActivationFunctionType

P = 128
SLOTS = 4
GROUP = P * SLOTS
D_GROUPS = D // GROUP
Y_GROUPS = MU // GROUP
HALF = MV // 2
QUARTER = MV // 4
F_WORDS = GROUP // 2
F_SLOT_BYTES = 2 * P
SCALE_WORDS = GROUP // 4
QUADRANT = 32
STAGE_BUFS = 5
E_LOADS = ((0, 0, 1), (0, 1, 2), (0, 2, 3), (1, 0, 1), (1, 1, 2), (1, 2, 3), (2, 0, 1), (2, 1, 3))
Y_PIECES = ((0, 0, HALF), (0, HALF, MV), (1, 0, MV))


def tile_cross_block_rayleigh_coefficients_k1_kernel(
    tc, x_words, x_scales, f_words, f_scales, E, w, U, gain, out_0, out_1, out_2
):
    nc = tc.nc
    with ExitStack() as ctx:
        keep = ctx.enter_context(tc.tile_pool(name="keep", bufs=1))
        stage = ctx.enter_context(tc.tile_pool(name="stage", bufs=STAGE_BUFS))
        psum = ctx.enter_context(tc.psum_pool(name="psum", bufs=8))
        ctx.enter_context(tc.manual_schedule())

        def kept(shape, dtype, name):
            return keep.tile(shape, dtype, name=name, align_bytes=64)

        def mx_operand(width, name):
            return kept([P, width], U32, name + "_codes"), kept([P, width], U8, name + "_scales")

        def weight_words():
            return stage.tile([P, GROUP * SLOTS], BF16, name="weight_words", align_bytes=64)

        def half_words():
            return stage.tile([P, HALF, SLOTS], BF16, name="half_words", align_bytes=64)

        def new_bank(shape, dtype):
            return psum.tile(shape, dtype, name="bank")

        groups = range(D_GROUPS)
        halves = range(2)
        slots = range(SLOTS)

        ident = kept([P, P], BF16, "ident")
        w_raw = kept([D_GROUPS, GROUP], BF16, "w_raw")
        w_rows = kept([P, GROUP], BF16, "w_rows")
        w_col = kept([P, SLOTS, D_GROUPS], F32, "w_col")
        gain_raw = kept([P, Y_GROUPS, SLOTS], BF16, "gain_raw")
        gain_col = kept([P, Y_GROUPS, SLOTS], F32, "gain_col")
        f_raw = [kept([P, D_GROUPS, F_WORDS], I32, "f_raw%d" % b) for b in groups]
        f_codes = [kept([P, D_GROUPS, 4 * F_WORDS], U8, "f_codes%d" % b) for b in groups]
        f_planes_raw = kept([P, D_GROUPS, D // 4], I32, "f_planes_raw")
        f_planes = [kept([P, D_GROUPS, GROUP], U8, "f_planes%d" % b) for b in groups]
        x_codes = [kept([P, D_GROUPS, HALF], U32, "x_codes%d" % h) for h in halves]
        x_planes = kept([P, D_GROUPS, MV], U8, "x_planes")
        e_rows = {ld: kept([P, SLOTS, GROUP * (ld[2] - ld[1])], BF16, "e_rows%d%d%d" % ld) for ld in E_LOADS}
        u_rows = [kept([P, SLOTS, MU], BF16, "u_rows%d" % g) for g in groups]
        pick_mx = mx_operand(GROUP, "pick")
        e_mx = {(g, b): mx_operand(GROUP, "e%d%d" % (g, b)) for g in groups for b in groups}
        u_mx = {(g, i): mx_operand(GROUP, "u%d%d" % (g, i)) for g in groups for i in range(Y_GROUPS)}
        z1_mx = {(b, h): mx_operand(HALF, "z1%d%d" % (b, h)) for b in groups for h in halves}
        z_mx = [mx_operand(MV, "z%d" % b) for b in groups]
        w_z1 = {(b, h): kept([P, SLOTS, HALF], F32, "w_z1%d%d" % (b, h)) for b in groups for h in halves}
        y = {pc[:2]: kept([P, SLOTS, pc[2] - pc[1]], F32, "y%d%d" % pc[:2]) for pc in Y_PIECES}
        y_codes = {(i, h): kept([P, HALF], U32, "y_codes%d%d" % (i, h)) for i in range(Y_GROUPS) for h in halves}
        y_planes = kept([P, MV], U8, "y_planes")
        pick_words = weight_words()
        staged = {}

        nc.gpsimd.dma_start(out=w_raw[:], in_=w.rearrange("(g k) -> g k", g=D_GROUPS))
        make_identity(nc, ident[:])
        nc.vector.memset(x_planes[:].bitcast(I32), 0)
        nc.vector.memset(f_planes_raw[:], 0)
        nc.vector.memset(pick_words[:], 0.0)
        nc.vector.memset(w_rows[:], 0.0)

        f_words32 = f_words.bitcast(I32).rearrange("g p n -> p g n")
        x_words32 = x_words.rearrange("g p n t -> g p (n t)").bitcast(I32).rearrange("g p n -> p g n")
        f_scales32 = f_scales.bitcast(I32).rearrange("g (q r) n -> r q g n", r=4)
        x_scales32 = x_scales.bitcast(I32).rearrange("g (q r) n -> r q g n", r=4)

        def load_f(b):
            nc.sync.dma_start(out=f_raw[b][:], in_=f_words32[:, :, F_WORDS * b : F_WORDS * (b + 1)])

        def load_x(h):
            nc.sync.dma_start(out=x_codes[h][:].bitcast(I32), in_=x_words32[:, :, HALF * h : HALF * (h + 1)])

        def load_rows(dst, src, g, col0, col1):
            rows = src[GROUP * g : GROUP * (g + 1), col0:col1].rearrange("(a t b) c -> t a b c", t=SLOTS, b=4)
            for t in slots:
                nc.sync.dma_start(out=dst[:, t, :], in_=rows[t])

        def load_e(ld):
            load_rows(e_rows[ld], E, ld[0], GROUP * ld[1], GROUP * ld[2])

        load_f(0)
        load_x(0)
        for r in range(4):
            queue = nc.sync if r < 2 else nc.gpsimd
            queue.dma_start(out=x_planes[:].bitcast(I32)[r:P:QUADRANT, :, :], in_=x_scales32[r])
        for r in range(4):
            nc.sync.dma_start(out=f_planes_raw[r:P:QUADRANT, :, :], in_=f_scales32[r])
        for ld in E_LOADS[0:3]:
            load_e(ld)
        load_x(1)
        load_f(1)
        for ld in E_LOADS[3:5]:
            load_e(ld)
        load_f(2)
        for ld in E_LOADS[5:]:
            load_e(ld)
        for g in groups:
            load_rows(u_rows[g], U, g, 0, MU)
        nc.sync.dma_start(out=gain_raw[:], in_=gain.rearrange("(i p t) -> p i t", p=P, t=SLOTS))

        def quantize(codes, scales, words):
            nc.vector.quantize_mx(out=codes.bitcast(FP8X4), scales=scales, in_=words)

        def copy_on(engine, out, in_):
            if engine == "vector":
                nc.vector.tensor_copy(out=out, in_=in_)
            else:
                nc.scalar.copy(out=out, in_=in_)

        def mx_pass(out, weights, t, codes, scales, start, stop):
            nc.tensor.matmul_mx(
                out=out,
                lhsT=weights[0][:, P * t : P * (t + 1)].bitcast(FP8X4),
                lhsT_scale=weights[1][:, P * t : P * (t + 1)],
                rhs=codes.bitcast(FP8X4),
                rhs_scale=scales,
                start=start,
                stop=stop,
            )

        def make_pick():
            nc.vector.tensor_copy(
                out=pick_words[:].rearrange("p (t a e) -> p t a e", t=SLOTS, e=16)[:, :, :, 0:16:5],
                in_=ident[:].rearrange("p (a t) -> p t a", t=SLOTS).unsqueeze(3).to_broadcast([P, SLOTS, 32, 4]),
            )
            quantize(pick_mx[0][:], pick_mx[1][:], pick_words[:])

        def sort_w():
            nc.scalar.activation(
                out=w_rows[0:D_GROUPS, :].rearrange("p (t a b) -> p t a b", t=SLOTS, b=4),
                in_=w_raw[:].rearrange("p (a t b) -> p t a b", t=SLOTS, b=4),
                func=ACT.Copy,
            )

        def turn_w():
            turned = new_bank([P, SLOTS, P], BF16)
            for t in slots:
                nc.tensor.transpose(turned[:, t, :], w_rows[:, P * t : P * (t + 1)], ident[:])
            nc.scalar.copy(out=w_col[:], in_=turned[:, :, 0:D_GROUPS])

        def sort_f_codes(b):
            nc.vector.tensor_copy(
                out=f_codes[b][:].bitcast(I32).rearrange("p g (t a v) -> p g t a v", t=SLOTS, v=2),
                in_=f_raw[b][:].rearrange("p g (a t v) -> p g t a v", t=SLOTS, v=2),
            )

        def sort_f_planes(b):
            raw = f_planes_raw[:, :, SCALE_WORDS * b : SCALE_WORDS * (b + 1)]
            nc.vector.tensor_copy(
                out=f_planes[b][:].bitcast(I32).rearrange("p g (t c m) -> p g c t m", t=SLOTS, m=4),
                in_=raw.rearrange("p g (c m t) -> p g c t m", t=SLOTS, m=4),
            )

        def sort_f(b):
            sort_f_codes(b)
            sort_f_planes(b)

        def lay_e(engine, g, b):
            ld = [x for x in E_LOADS if x[0] == g and x[1] <= b < x[2]][0]
            rows = e_rows[ld][:, :, GROUP * (b - ld[1]) : GROUP * (b - ld[1] + 1)]
            staged["e", g, b] = weight_words()
            copy_on(
                engine,
                staged["e", g, b][:].rearrange("p (t a b j) -> p t a j b", t=SLOTS, b=4, j=SLOTS),
                rows.rearrange("p j (a t b) -> p t a j b", t=SLOTS, b=4),
            )

        def quant_e(g, b):
            quantize(e_mx[g, b][0][:], e_mx[g, b][1][:], staged["e", g, b][:])

        def lay_u(engine, g, i, t0=0, t1=SLOTS):
            if t0 == 0:
                staged["u", g, i] = weight_words()
            dst = staged["u", g, i][:].rearrange("p (t m j) -> p m j t", t=SLOTS, j=SLOTS)
            src = u_rows[g][:, :, GROUP * i : GROUP * (i + 1)].rearrange("p j (m t) -> p m j t", t=SLOTS)
            copy_on(engine, dst[:, :, :, t0:t1], src[:, :, :, t0:t1])

        def quant_u(g, i):
            quantize(u_mx[g, i][0][:], u_mx[g, i][1][:], staged["u", g, i][:])

        def first_product(b, h):
            z1_words = half_words()
            staged["z1", b, h] = z1_words
            for q in range(2):
                cols = slice(QUARTER * q, QUARTER * (q + 1))
                x_cols = slice(HALF * h + cols.start, HALF * h + cols.stop)
                bank = new_bank([P, SLOTS, QUARTER], F32)
                for t in slots:
                    for g in groups:
                        nc.tensor.matmul_mx(
                            out=bank[:, t, :],
                            lhsT=f_codes[b][:, g, F_SLOT_BYTES * t : F_SLOT_BYTES * (t + 1)].bitcast(FP4X4),
                            lhsT_scale=f_planes[b][:, g, P * t : P * (t + 1)],
                            rhs=x_codes[h][:, g, cols].bitcast(FP8X4),
                            rhs_scale=x_planes[:, g, x_cols],
                            start=(g == 0),
                            stop=False,
                        )
                    mx_pass(bank[:, t, :], pick_mx, t, x_codes[h][:, b, cols], x_planes[:, b, x_cols], False, True)
                nc.scalar.copy(out=z1_words[:, cols, :], in_=bank[:].rearrange("p t n -> p n t"))
                if (b, h, q) == (0, 0, 0):
                    turn_w()
                for t in slots:
                    nc.scalar.activation(
                        out=w_z1[b, h][:, t, cols], in_=bank[:, t, :], func=ACT.Copy, scale=w_col[:, t, b : b + 1]
                    )

        def quant_z1(b, h):
            quantize(z1_mx[b, h][0][:], z1_mx[b, h][1][:], staged["z1", b, h][:].rearrange("p n t -> p (n t)"))

        def second_product(b, h):
            for t in slots:
                if t % 2 == 0:
                    bank = new_bank([P, 2, HALF], F32)
                staged["ez1", b, h, t] = bank[:, t % 2, :]
                for g in groups:
                    codes, scales = z1_mx[g, h]
                    mx_pass(bank[:, t % 2, :], e_mx[g, b], t, codes[:], scales[:], g == 0, g == D_GROUPS - 1)

        def finish_z(b, h):
            z_slots = stage.tile([P, SLOTS, HALF], BF16, name="z_slots", bufs=2, align_bytes=64)
            staged["z_slots", b, h] = z_slots
            for t in slots:
                nc.vector.scalar_tensor_tensor(
                    out=z_slots[:, t, :],
                    in0=staged["ez1", b, h, t],
                    scalar=w_col[:, t, b : b + 1],
                    in1=w_z1[b, h][:, t, :],
                    op0=ALU.mult,
                    op1=ALU.add,
                )

        def lay_slots(engine, key, by_slot):
            staged[key] = half_words()
            copy_on(
                engine,
                staged[key][:].rearrange("p (c n) t -> p c t n", n=4),
                by_slot.rearrange("p t (c n) -> p c t n", n=4),
            )

        def lay_z(b, h):
            lay_slots("vector", ("z", b, h), staged["z_slots", b, h][:])

        def quant_z(b, h):
            cols = slice(HALF * h, HALF * (h + 1))
            quantize(z_mx[b][0][:, cols], z_mx[b][1][:, cols], staged["z", b, h][:].rearrange("p n t -> p (n t)"))

        def third_product(piece, g0=0, g1=D_GROUPS):
            i, col0, col1 = piece
            for t in slots:
                if g1 - g0 == D_GROUPS:
                    if t % 2 == 0:
                        bank = new_bank([P, 2, col1 - col0], F32)
                    staged["uz", piece, t] = bank[:, t % 2, :]
                elif g0 == 0:
                    bank = new_bank([P, col1 - col0], F32)
                    staged["uz", piece, t] = bank[:]
                for g in range(g0, g1):
                    codes, scales = z_mx[g][0][:, col0:col1], z_mx[g][1][:, col0:col1]
                    mx_pass(staged["uz", piece, t], u_mx[g, i], t, codes, scales, g == 0, g == D_GROUPS - 1)

        def finish_y(engine, piece, t0, t1):
            i, col0, col1 = piece
            for t in range(t0, t1):
                out, sums, factor = y[i, col0][:, t, :], staged["uz", piece, t], gain_col[:, i, t : t + 1]
                if engine == "vector":
                    nc.vector.tensor_scalar(out=out, in0=sums, scalar1=factor, scalar2=None, op0=ALU.mult)
                else:
                    nc.scalar.activation(out=out, in_=sums, func=ACT.Copy, scale=factor)
            rows = out_0[GROUP * i : GROUP * (i + 1), col0:col1].rearrange("(p t) m -> p t m", t=SLOTS)
            nc.sync.dma_start(out=rows[:, t0:t1, :], in_=y[i, col0][:, t0:t1, :])

        def lay_y(engine, i, h):
            col0 = [pc[1] for pc in Y_PIECES if pc[0] == i and pc[1] <= HALF * h < pc[2]][0]
            lay_slots(engine, ("y", i, h), y[i, col0][:, :, HALF * h - col0 : HALF * (h + 1) - col0])

        def quant_y(i, h):
            cols = slice(HALF * h, HALF * (h + 1))
            quantize(y_codes[i, h][:], y_planes[4 * i : P, cols], staged["y", i, h][:].rearrange("p n t -> p (n t)"))
            nc.sync.dma_start(
                out=out_1[i].rearrange("p n t -> p (n t)").bitcast(I32)[:, cols], in_=y_codes[i, h][:].bitcast(I32)
            )

        sort_f_codes(0)
        make_pick()
        sort_f_planes(0)
        sort_w()
        lay_e("scalar", 0, 1)

        first_product(0, 0)
        lay_e("vector", 0, 0)
        quant_e(0, 0)

        first_product(0, 1)
        lay_e("vector", 0, 2)
        quant_e(0, 1)
        quant_e(0, 2)
        sort_f(1)
        quant_z1(0, 0)

        first_product(1, 0)
        lay_e("vector", 1, 0)
        quant_e(1, 0)
        quant_z1(0, 1)

        first_product(1, 1)
        lay_e("vector", 1, 1)
        sort_f(2)
        quant_e(1, 1)
        lay_e("vector", 1, 2)
        quant_z1(1, 0)
        quant_e(1, 2)

        first_product(2, 0)
        lay_e("vector", 2, 0)
        quant_z1(1, 1)
        quant_e(2, 0)

        first_product(2, 1)
        lay_e("scalar", 2, 2)
        lay_e("vector", 2, 1)
        quant_z1(2, 0)
        quant_e(2, 1)

        z_parts = [(0, 0), (1, 0), (0, 1), (1, 1), (2, 0), (2, 1)]
        z_finish = [(0, 0), (1, 0), (0, 1), (2, 0), (1, 1), (2, 1)]
        u_pieces = [(g, i) for i in range(Y_GROUPS) for g in groups]
        y_left, y_right, y_last = Y_PIECES

        second_product(*z_parts[0])
        second_product(*z_parts[1])
        quant_z1(2, 1)
        for n in range(len(z_finish)):
            if n < len(u_pieces) - 1:
                lay_u("scalar", *u_pieces[n])
            finish_z(*z_finish[n])
            if n > 0:
                quant_z(*z_finish[n - 1])
            if n == 1:
                quant_e(2, 2)
            if n > 1:
                quant_u(*u_pieces[n - 2])
            if n + 2 < len(z_parts):
                second_product(*z_parts[n + 2])
            if z_finish[n - 1] == (2, 0):
                third_product(y_left)
            lay_z(*z_finish[n])

        third_product(y_last, 0, 1)
        nc.scalar.copy(out=gain_col[:], in_=gain_raw[:])
        finish_y("scalar", y_left, 0, SLOTS)
        quant_u(1, 1)
        quant_z(2, 1)
        third_product(y_right)
        third_product(y_last, 1, 2)
        lay_u("scalar", 2, 1, 0, 2)
        lay_u("vector", 2, 1, 2, SLOTS)
        lay_y("vector", 0, 0)
        quant_u(2, 1)
        third_product(y_last, 2, D_GROUPS)
        finish_y("scalar", y_right, 0, 2)
        finish_y("scalar", y_right, 2, SLOTS)
        quant_y(0, 0)
        lay_y("vector", 0, 1)
        finish_y("scalar", y_last, 0, 2)
        finish_y("vector", y_last, 2, SLOTS)
        quant_y(0, 1)
        lay_y("scalar", 1, 1)
        lay_y("vector", 1, 0)
        quant_y(1, 0)
        quant_y(1, 1)
        for q in range(4):
            nc.scalar.dma_start(
                out=out_2.bitcast(I32)[:, 4 * q : 4 * (q + 1), :],
                in_=y_planes[QUADRANT * q : QUADRANT * q + 4 * Y_GROUPS, :].bitcast(I32),
            )
